import numpy as np
import ml_dtypes


def mxq(x, axis, fmt="e4m3"):
    dtype, down = {"e4m3": (ml_dtypes.float8_e4m3fn, 7), "e5m2": (ml_dtypes.float8_e5m2, 14)}[fmt]
    v = np.moveaxis(np.asarray(x, np.float32).astype(ml_dtypes.bfloat16).astype(np.float64), axis, -1)
    blocks = v.reshape(v.shape[:-1] + (-1, 32))
    amax = np.abs(blocks).max(-1, keepdims=True)
    byte = np.maximum(np.where(amax > 0, np.frexp(amax)[1] - 1 + 127, 0) - down, 1)
    scale = np.exp2(byte - 127.0)
    codes = (blocks / scale).astype(np.float32).astype(dtype).astype(np.float64)
    return np.moveaxis((codes * scale).reshape(v.shape), -1, axis)


WIDE = False


def mx_kscale(k):
    if not WIDE:
        return np.ones(k)
    levels = np.array([10, -10, 5, -5, 0])
    if k % 512:
        return np.exp2(np.random.permutation(np.resize(levels, k // 32))).repeat(32)
    a = np.empty((k // 512, 16))
    for p in range(k // 512):
        a[p, :8] = np.random.permutation(np.resize(levels, 8))
        for g in range(8):
            far = levels[np.abs(levels - a[p, g]) >= 10]
            a[p, g + 8] = far[np.random.randint(len(far))]
    return np.exp2(a.ravel()).repeat(32)


def f64(x):
    return np.asarray(x).astype(np.float64)


def striped(idx):
    return np.tile(idx.reshape(-1, 16).T, (8, 1)).astype(np.uint16)


def unstriped(offs):
    return offs[:16].T.reshape(-1).astype(np.int64)


def striped8(idx):
    return np.concatenate([x.reshape(-1, 16).T for x in idx]).astype(np.uint16)


def runs(offs, k):
    lists = np.stack([offs[16 * r : 16 * r + 16].T.reshape(-1) for r in range(8)]).astype(np.int64)
    return lists[np.arange(k) % 512 // 64]


def pack_weight(w):
    k, n = w.shape
    w = f64(np.asarray(w, np.float32).astype(ml_dtypes.bfloat16)).reshape(k // 32, 32, n)
    amax = np.abs(w).max(1)
    byte = np.clip(np.where(amax > 0, np.frexp(amax)[1] - 1 + 127 - 7, 1), 1, 254)
    scaled = (w * np.exp2(127.0 - byte)[:, None, :]).reshape(k, n).astype(np.float32)
    words = np.ascontiguousarray(scaled.reshape(k // 512, 128, 4, n).transpose(0, 1, 3, 2)).astype(ml_dtypes.float8_e4m3fn).view(np.uint8)
    return words, np.ascontiguousarray(byte.astype(np.uint8).reshape(k // 512, 16, n))


def unpack_weight(words, scales):
    g, p, n, _ = words.shape
    vals = np.ascontiguousarray(words).view(ml_dtypes.float8_e4m3fn).astype(np.float64) * np.repeat(np.exp2(scales.astype(np.float64) - 127.0), 8, axis=1)[..., None]
    return vals.transpose(0, 1, 3, 2).reshape(g * 512, n)


def sigmoid(v):
    return 1.0 / (1.0 + np.exp(-np.maximum(v, -700.0)))


K, T, S, N, H = 512, 2048, 512, 512, 512


def setup_inputs():
    n = np.random.standard_normal
    s = mx_kscale(K)[:, None]
    u = mx_kscale(H)
    packed_xT = pack_weight(n((K, T)) * s)
    return {
        "x_words": packed_xT[0],
        "x_scales": packed_xT[1],
        "w1": (n((K, H)) / np.sqrt(K) / s).astype(np.float32),
        "w2": (n((K, H)) / np.sqrt(K) / s).astype(np.float32),
        "w3": (n((K, H)) / np.sqrt(K) / s).astype(np.float32),
        "gn": (np.random.uniform(0.5, 1.5, (H, 1)) * u[:, None]).astype(np.float32),
        "w4": (n((H, N)) / np.sqrt(H) / u[:, None]).astype(np.float32),
        "offs": striped(np.random.permutation(T)[:S]),
        "two": striped(np.random.permutation(T)[:S]),
        "three": striped(np.random.permutation(T)[:S]),
        "n1": striped8(np.stack([np.random.permutation(S) for _ in range(8)])),
        "n2": striped8(np.stack([np.random.permutation(S) for _ in range(8)])),
        "n3": striped8(np.stack([np.random.permutation(S) for _ in range(8)])),
        "n4": striped8(np.stack([np.random.permutation(S) for _ in range(8)])),
        "n5": striped8(np.stack([np.random.permutation(S) for _ in range(8)])),
        "n6": striped8(np.stack([np.random.permutation(S) for _ in range(8)])),
    }


def reference(x_words, x_scales, w1, w2, w3, gn, w4, offs, two, three, n1, n2, n3, n4, n5, n6):
    xq = unpack_weight(x_words, x_scales)[:, unstriped(offs)]
    y = mxq(f64(w1), 0, "e4m3").T @ xq
    x_two = unpack_weight(x_words, x_scales)[:, unstriped(two)]
    d = mxq(f64(w2), 0, "e4m3").T @ x_two
    m1 = y + (sigmoid(d[np.arange(H)[:, None], runs(n2, H)] - d)) * (y[np.arange(H)[:, None], runs(n1, H)] - y)
    x_three = unpack_weight(x_words, x_scales)[:, unstriped(three)]
    b = mxq(f64(w3), 0, "e4m3").T @ x_three
    z = f64(gn) * ((m1 + m1[np.arange(H)[:, None], runs(n3, H)]) * (sigmoid(b + b[np.arange(H)[:, None], runs(n4, H)])))
    h = mxq(f64(w4), 0, "e4m3").T @ mxq(z, 0, "e4m3")
    pa = h[np.arange(N)[:, None], runs(n5, N)]
    pb = h[np.arange(N)[:, None], runs(n6, N)]
    mu = 0.3125 * (h + pa + pb)
    return (h - mu) / (np.sqrt((pa - mu) ** 2 + (pb - mu) ** 2 + 0.25))

@@ -1,0 +1,244 @@
+import math
+from contextlib import ExitStack
+
+import concourse.mybir as mybir
+
+F32 = mybir.dt.float32
+BF16 = mybir.dt.bfloat16
+I32 = mybir.dt.int32
+U32 = mybir.dt.uint32
+U16 = mybir.dt.uint16
+U8 = mybir.dt.uint8
+FP8X4 = mybir.dt.float8_e4m3fn_x4
+ACT = mybir.ActivationFunctionType
+ALU = mybir.AluOpType
+
+P = 128
+PACK = 4
+T = 2048
+S = 512
+WIN = 2 * S
+HALF = S // 2
+FLOPS = 4 * 2 * 512 * 512 * 512
+
+
+def tile_picked_triopullbtriebstd_none_p_kernel(tc, x_words, x_scales, w1, w2, w3, gn, w4, offs, two, three, n1, n2, n3, n4, n5, n6, out):
+    nc = tc.nc
+    with ExitStack() as ctx:
+        keep = ctx.enter_context(tc.tile_pool(name="keep", bufs=1))
+        work = ctx.enter_context(tc.tile_pool(name="work", bufs=2))
+        psum = ctx.enter_context(tc.psum_pool(name="psum", bufs=8))
+
+        def list_tile(name):
+            return keep.tile([P, S // 16], U16, name=name)
+
+        l_offs, l_two, l_three = list_tile("l_offs"), list_tile("l_two"), list_tile("l_three")
+        l1, l2, l3 = list_tile("l1"), list_tile("l2"), list_tile("l3")
+        l4, l5, l6 = list_tile("l4"), list_tile("l5"), list_tile("l6")
+
+        xw = keep.tile([P, T], U32, name="xw", align_bytes=64)
+        xs = keep.tile([P, T], U8, name="xs", align_bytes=64)
+        gain = keep.tile([P, PACK], F32, name="gain")
+        quarter = keep.tile([P, 1], F32, name="quarter")
+        warm = keep.tile([P, 1], F32, name="warm")
+        warm2 = keep.tile([P, 1], F32, name="warm2")
+        raw = [keep.tile([P, PACK, S], F32, name="raw%d" % i) for i in range(4)]
+        wb = [keep.tile([P, PACK * S], BF16, name="wb%d" % i, align_bytes=64) for i in range(4)]
+        wc = [keep.tile([P, S], U32, name="wc%d" % i, align_bytes=64) for i in range(4)]
+        ws = [keep.tile([P, S], U8, name="ws%d" % i, align_bytes=64) for i in range(4)]
+        gw = [keep.tile([P, S], U32, name="gw%d" % i, align_bytes=64) for i in range(3)]
+        gs = [keep.tile([P, S], U8, name="gs%d" % i, align_bytes=64) for i in range(3)]
+        win_a = [keep.tile([P, WIN], F32, name="wa%d" % t) for t in range(PACK)]
+        win_y = [keep.tile([P, WIN], F32, name="wy%d" % t) for t in range(PACK)]
+        win_b = [keep.tile([P, WIN], F32, name="wb_%d" % t) for t in range(PACK)]
+        p_all = keep.tile([P, PACK, S], F32, name="p_all")
+        s2_all = keep.tile([P, PACK, S], F32, name="s2_all")
+        zb = keep.tile([P, S * PACK], BF16, name="zb", align_bytes=64)
+        zc = keep.tile([P, S], U32, name="zc", align_bytes=64)
+        zs = keep.tile([P, S], U8, name="zs", align_bytes=64)
+
+        nc.vector.memset(xs[:].bitcast(I32), 0)
+        nc.vector.memset(quarter[:], 0.25)
+        nc.sync.dma_start(l_two[:], two)
+        nc.sync.dma_start(l_offs[:], offs)
+        nc.sync.dma_start(l_three[:], three)
+        for q in range(4):
+            nc.scalar.dma_start(xs[32 * q : 32 * q + 4, :].bitcast(I32), x_scales[0, 4 * q : 4 * q + 4, :].bitcast(I32))
+        nc.scalar.activation(warm[:], quarter[:], ACT.Sigmoid)
+
+        def load_w(i, w):
+            nc.sync.dma_start(raw[i][:], w.rearrange("(p j) c -> p j c", j=PACK))
+
+        load_w(1, w2)
+        nc.sync.dma_start(xw[:].bitcast(I32), x_words[0].rearrange("p n t -> p (n t)").bitcast(I32))
+        load_w(0, w1)
+        nc.sync.dma_start(l2[:], n2)
+        nc.sync.dma_start(gain[:], gn.rearrange("(p t) o -> p (t o)", t=PACK))
+        nc.sync.dma_start(l1[:], n1)
+        load_w(2, w3)
+        nc.sync.dma_start(l4[:], n4)
+        nc.sync.dma_start(l3[:], n3)
+        load_w(3, w4)
+        nc.sync.dma_start(l5[:], n5)
+        nc.sync.dma_start(l6[:], n6)
+
+        for t in range(PACK):
+            nc.vector.memset(win_a[t][:, S:], 0.0)
+        for t in range(PACK):
+            nc.gpsimd.memset(win_y[t][:, S:], 0.0)
+        for t in range(2):
+            nc.vector.memset(win_b[t][:, S:], 0.0)
+        for t in range(2, PACK):
+            nc.gpsimd.memset(win_b[t][:, S:], 0.0)
+
+        def cast_w(i):
+            nc.scalar.copy(
+                wb[i][:].rearrange("p (t m j) -> p m t j", t=PACK, j=PACK),
+                raw[i][:].rearrange("p j (m t) -> p m t j", t=PACK),
+            )
+
+        def quant_w(i, c0=0, c1=S):
+            nc.vector.quantize_mx(wc[i][:, c0:c1].bitcast(FP8X4), ws[i][:, c0:c1], wb[i][:, PACK * c0 : PACK * c1])
+
+        def product(acc, i, t, words, scales):
+            cols = slice(P * t, P * (t + 1))
+            nc.tensor.matmul_mx(
+                out=acc, lhsT=wc[i][:, cols].bitcast(FP8X4), lhsT_scale=ws[i][:, cols],
+                rhs=words.bitcast(FP8X4), rhs_scale=scales, start=True, stop=True,
+            )
+
+        def gather_bytes(i, lst):
+            nc.vector.tensor_copy(gs[i][:], xs[:].indirect(lst[:]))
+
+        def gather_words(i, lst):
+            nc.vector.tensor_copy(gw[i][:], xw[:].indirect(lst[:]))
+
+        gather_bytes(1, l_two)
+        gather_bytes(0, l_offs)
+        gather_bytes(2, l_three)
+        cast_w(1)
+        gather_words(1, l_two)
+        quant_w(1)
+        gather_words(0, l_offs)
+
+        s1 = []
+
+        def stage_d(t):
+            acc = psum.tile([P, S], F32, name="acc")
+            product(acc[:], 1, t, gw[1][:], gs[1][:])
+            dc = work.tile([P, S], F32, name="dc")
+            nc.scalar.copy(win_a[t][:, :S], acc[:])
+            nc.scalar.copy(dc[:], acc[:])
+            u = work.tile([P, S], F32, name="u")
+            nc.vector.tensor_tensor(u[:], win_a[t][:].indirect(l2[:]), dc[:], ALU.subtract)
+            g = keep.tile([P, S], F32, name="s1_%d" % t)
+            nc.scalar.activation(g[:], u[:], ACT.Sigmoid)
+            s1.append(g)
+
+        m1c = []
+
+        def stage_y(t):
+            acc = psum.tile([P, S], F32, name="acc")
+            product(acc[:], 0, t, gw[0][:], gs[0][:])
+            nc.scalar.activation(win_y[t][:, :S], acc[:], ACT.Copy, scale=gain[:, t : t + 1])
+            near = work.tile([P, S], F32, name="near")
+            nc.vector.scalar_tensor_tensor(near[:], s1[t][:], 1.0, win_y[t][:, :S], ALU.subtract, ALU.mult)
+            far = work.tile([P, S], F32, name="far")
+            nc.vector.tensor_tensor(far[:], win_y[t][:].indirect(l1[:]), s1[t][:], ALU.mult)
+            nc.vector.tensor_tensor(win_a[t][:, :S], far[:], near[:], ALU.subtract)
+            c = work.tile([P, S], F32, name="m1c")
+            nc.scalar.copy(c[:], win_a[t][:, :S])
+            m1c.append(c)
+
+        def stage_b(t):
+            acc = psum.tile([P, S], F32, name="acc")
+            product(acc[:], 2, t, gw[2][:], gs[2][:])
+            bc = work.tile([P, S], F32, name="bc")
+            nc.scalar.copy(win_b[t][:, :S], acc[:])
+            nc.scalar.copy(bc[:], acc[:])
+            v = work.tile([P, S], F32, name="v")
+            nc.vector.tensor_tensor(v[:], win_b[t][:].indirect(l4[:]), bc[:], ALU.add)
+            nc.scalar.activation(s2_all[:, t, :], v[:], ACT.Sigmoid)
+
+        def stage_p(t):
+            nc.vector.tensor_tensor(p_all[:, t, :], win_a[t][:].indirect(l3[:]), m1c[t][:], ALU.add)
+
+        stage_d(0)
+        cast_w(0)
+        quant_w(0)
+        gather_words(2, l_three)
+        stage_d(1)
+        stage_d(2)
+        stage_y(0)
+        stage_d(3)
+        cast_w(2)
+        quant_w(2)
+        stage_y(1)
+        stage_p(0)
+        stage_b(0)
+        stage_y(2)
+        stage_p(1)
+        stage_b(1)
+        cast_w(3)
+        stage_y(3)
+        stage_p(2)
+        stage_b(2)
+        quant_w(3, 0, P)
+        stage_b(3)
+        stage_p(3)
+        nc.scalar.activation(warm2[:], s2_all[:, PACK - 1, 0:1], ACT.Abs_reciprocal_sqrt)
+
+        for c0 in (0, HALF):
+            nc.vector.tensor_tensor(
+                zb[:, PACK * c0 : PACK * (c0 + HALF)].rearrange("p (c i t) -> p c t i", i=4, t=PACK),
+                p_all[:, :, c0 : c0 + HALF].rearrange("p t (c i) -> p c t i", i=4),
+                s2_all[:, :, c0 : c0 + HALF].rearrange("p t (c i) -> p c t i", i=4),
+                ALU.mult,
+            )
+        for c0 in (0, HALF):
+            nc.vector.quantize_mx(zc[:, c0 : c0 + HALF].bitcast(FP8X4), zs[:, c0 : c0 + HALF], zb[:, PACK * c0 : PACK * (c0 + HALF)])
+        for t in range(1, PACK):
+            quant_w(3, P * t, P * (t + 1))
+
+        rows = out.rearrange("(p t) s -> p t s", t=PACK)
+        for t in range(PACK):
+            acc = psum.tile([P, S], F32, name="acc")
+            for c0 in (0, HALF):
+                product(acc[:, c0 : c0 + HALF], 3, t, zc[:, c0 : c0 + HALF], zs[:, c0 : c0 + HALF])
+            nc.scalar.copy(win_b[t][:, :S], acc[:])
+
+        held = []
+
+        def head(t):
+            h = win_b[t]
+            pa = work.tile([P, S], F32, name="pa")
+            nc.vector.tensor_copy(pa[:], h[:].indirect(l5[:]))
+            both = work.tile([P, S], F32, name="both")
+            nc.vector.tensor_tensor(both[:], h[:].indirect(l6[:]), pa[:], ALU.add)
+            diff = work.tile([P, S], F32, name="diff")
+            nc.vector.scalar_tensor_tensor(diff[:], pa[:], 2.0, both[:], ALU.mult, ALU.subtract)
+            mid = work.tile([P, S], F32, name="mid")
+            nc.vector.scalar_tensor_tensor(mid[:], h[:, :S], -5.0 / 3.0, both[:], ALU.mult, ALU.add)
+            num = work.tile([P, S], F32, name="num")
+            nc.vector.scalar_tensor_tensor(num[:], h[:, :S], 11.0 / 5.0, both[:], ALU.mult, ALU.subtract)
+            sq_d = work.tile([P, S], F32, name="sq_d")
+            nc.scalar.activation(sq_d[:], diff[:], ACT.Square, scale=math.sqrt(0.5))
+            sq_m = work.tile([P, S], F32, name="sq_m")
+            nc.scalar.activation(sq_m[:], mid[:], ACT.Square, scale=3.0 / 16.0 * math.sqrt(2.0))
+            held.append((num, sq_d, sq_m))
+
+        def tail(t):
+            num, sq_d, sq_m = held[t]
+            q = work.tile([P, S], F32, name="q")
+            nc.vector.tensor_tensor(q[:], sq_d[:], sq_m[:], ALU.add)
+            r = work.tile([P, S], F32, name="r")
+            nc.scalar.activation(r[:], q[:], ACT.Abs_reciprocal_sqrt, bias=quarter[:])
+            res = work.tile([P, S], F32, name="res")
+            nc.vector.scalar_tensor_tensor(res[:], num[:], 0.3125, r[:], ALU.mult, ALU.mult)
+            nc.sync.dma_start(rows[:, t, :], res[:])
+
+        head(0)
+        for t in range(1, PACK):
+            head(t)
+            tail(t - 1)
+        tail(PACK - 1)

@@ -2,6 +2,7 @@ import math
 from contextlib import ExitStack
 
 import concourse.mybir as mybir
+from concourse.masks import make_identity
 
 F32 = mybir.dt.float32
 BF16 = mybir.dt.bfloat16
@@ -27,7 +28,7 @@ def tile_picked_triopullbtriebstd_none_p_kernel(tc, x_words, x_scales, w1, w2, w
     with ExitStack() as ctx:
         keep = ctx.enter_context(tc.tile_pool(name="keep", bufs=1))
         work = ctx.enter_context(tc.tile_pool(name="work", bufs=2))
-        psum = ctx.enter_context(tc.psum_pool(name="psum", bufs=8))
+        psum = ctx.enter_context(tc.psum_pool(name="psum", bufs=4))
 
         def list_tile(name):
             return keep.tile([P, S // 16], U16, name=name)
@@ -42,35 +43,34 @@ def tile_picked_triopullbtriebstd_none_p_kernel(tc, x_words, x_scales, w1, w2, w
         quarter = keep.tile([P, 1], F32, name="quarter")
         warm = keep.tile([P, 1], F32, name="warm")
         warm2 = keep.tile([P, 1], F32, name="warm2")
-        raw = [keep.tile([P, PACK, S], F32, name="raw%d" % i) for i in range(4)]
+        raw = [[keep.tile([P, PACK, HALF], F32, name="raw%d_%d" % (i, a)) for a in range(2)] for i in range(4)]
+        ident = keep.tile([P, P], F32, name="ident")
         wb = [keep.tile([P, PACK * S], BF16, name="wb%d" % i, align_bytes=64) for i in range(4)]
         wc = [keep.tile([P, S], U32, name="wc%d" % i, align_bytes=64) for i in range(4)]
         ws = [keep.tile([P, S], U8, name="ws%d" % i, align_bytes=64) for i in range(4)]
-        gw = [keep.tile([P, S], U32, name="gw%d" % i, align_bytes=64) for i in range(3)]
+        gw = [keep.tile([P, S], U32, name="gw%d" % i, align_bytes=64) for i in range(2)]
+        win_b = [keep.tile([P, WIN], F32, name="wb_%d" % t) for t in range(PACK)]
         gs = [keep.tile([P, S], U8, name="gs%d" % i, align_bytes=64) for i in range(3)]
         win_a = [keep.tile([P, WIN], F32, name="wa%d" % t) for t in range(PACK)]
         win_y = [keep.tile([P, WIN], F32, name="wy%d" % t) for t in range(PACK)]
-        win_b = [keep.tile([P, WIN], F32, name="wb_%d" % t) for t in range(PACK)]
-        p_all = keep.tile([P, PACK, S], F32, name="p_all")
-        s2_all = keep.tile([P, PACK, S], F32, name="s2_all")
+        z_rows = keep.tile([P, PACK, S], BF16, name="z_rows")
         zb = keep.tile([P, S * PACK], BF16, name="zb", align_bytes=64)
         zc = keep.tile([P, S], U32, name="zc", align_bytes=64)
         zs = keep.tile([P, S], U8, name="zs", align_bytes=64)
 
-        nc.vector.memset(xs[:].bitcast(I32), 0)
-        nc.vector.memset(quarter[:], 0.25)
+        for q in range(4):
+            rows4 = x_scales[0, 4 * q : 4 * q + 4, :].bitcast(I32).rearrange("r c -> (r c)")
+            nc.sync.dma_start(xs[32 * q : 32 * (q + 1), :].bitcast(I32), rows4.partition_broadcast(8))
         nc.sync.dma_start(l_two[:], two)
         nc.sync.dma_start(l_offs[:], offs)
         nc.sync.dma_start(l_three[:], three)
-        for q in range(4):
-            nc.scalar.dma_start(xs[32 * q : 32 * q + 4, :].bitcast(I32), x_scales[0, 4 * q : 4 * q + 4, :].bitcast(I32))
-        nc.scalar.activation(warm[:], quarter[:], ACT.Sigmoid)
+        nc.sync.dma_start(xw[:].bitcast(I32), x_words[0].rearrange("p n t -> p (n t)").bitcast(I32))
 
         def load_w(i, w):
-            nc.sync.dma_start(raw[i][:], w.rearrange("(p j) c -> p j c", j=PACK))
+            for a in range(2):
+                nc.sync.dma_start(raw[i][a][:], w.rearrange("(p j) c -> p j c", j=PACK)[:, :, a * HALF : (a + 1) * HALF])
 
         load_w(1, w2)
-        nc.sync.dma_start(xw[:].bitcast(I32), x_words[0].rearrange("p n t -> p (n t)").bitcast(I32))
         load_w(0, w1)
         nc.sync.dma_start(l2[:], n2)
         nc.sync.dma_start(gain[:], gn.rearrange("(p t) o -> p (t o)", t=PACK))
@@ -82,20 +82,24 @@ def tile_picked_triopullbtriebstd_none_p_kernel(tc, x_words, x_scales, w1, w2, w
         nc.sync.dma_start(l5[:], n5)
         nc.sync.dma_start(l6[:], n6)
 
-        for t in range(PACK):
-            nc.vector.memset(win_a[t][:, S:], 0.0)
+        nc.vector.memset(quarter[:], 0.25)
+        nc.scalar.activation(warm[:], quarter[:], ACT.Sigmoid)
         for t in range(PACK):
             nc.gpsimd.memset(win_y[t][:, S:], 0.0)
-        for t in range(2):
+        for t in range(PACK):
             nc.vector.memset(win_b[t][:, S:], 0.0)
-        for t in range(2, PACK):
-            nc.gpsimd.memset(win_b[t][:, S:], 0.0)
+        for t in range(PACK):
+            nc.scalar.copy(win_a[t][:, S:], win_y[0][:, S:])
+        make_identity(nc, ident[:])
 
-        def cast_w(i):
-            nc.scalar.copy(
-                wb[i][:].rearrange("p (t m j) -> p m t j", t=PACK, j=PACK),
-                raw[i][:].rearrange("p j (m t) -> p m t j", t=PACK),
-            )
+        def cast_w(i, *copies):
+            for a, copy in enumerate(copies):
+                if copy is None:
+                    continue
+                copy(
+                    wb[i][:].rearrange("p (t m j) -> p m t j", t=PACK, j=PACK)[:, a * P // 2 : (a + 1) * P // 2],
+                    raw[i][a][:].rearrange("p j (m t) -> p m t j", t=PACK),
+                )
 
         def quant_w(i, c0=0, c1=S):
             nc.vector.quantize_mx(wc[i][:, c0:c1].bitcast(FP8X4), ws[i][:, c0:c1], wb[i][:, PACK * c0 : PACK * c1])
@@ -113,132 +117,270 @@ def tile_picked_triopullbtriebstd_none_p_kernel(tc, x_words, x_scales, w1, w2, w
         def gather_words(i, lst):
             nc.vector.tensor_copy(gw[i][:], xw[:].indirect(lst[:]))
 
+        def new(name, bufs=2):
+            return work.tile([P, S], F32, name=name, bufs=bufs)
+
         gather_bytes(1, l_two)
         gather_bytes(0, l_offs)
         gather_bytes(2, l_three)
-        cast_w(1)
         gather_words(1, l_two)
-        quant_w(1)
         gather_words(0, l_offs)
+        cast_w(1, nc.scalar.copy, nc.scalar.copy)
+        quant_w(1)
+        gw.append(keep.tile([P, S], U32, name="wb1", align_bytes=64))
+        gather_words(2, l_three)
+        cast_w(0, nc.scalar.copy, nc.vector.tensor_copy)
+        quant_w(0)
 
-        s1 = []
+        def turned_sum(parts, name="turned"):
+            bank = psum.tile([P, S], F32, name=name)
+            for c0 in range(0, S, P):
+                for k, part in enumerate(parts):
+                    nc.tensor.matmul(
+                        bank[:, c0 : c0 + P], part[:, c0 : c0 + P], ident[:],
+                        start=(k == 0), stop=(k == len(parts) - 1), is_transpose=True,
+                    )
+            return bank
+
+        last = PACK - 1
+        NPE = 3
+        s1, s2, m1c, near, far, pair = {}, {}, {}, {}, {}, {}
+
+        u, v, bc, m1t, dc_, = {}, {}, {}, {}, {}
+        NM, NB = 3, 1
+
+        def second_copy(plain, window, bank, soon):
+            if soon:
+                nc.scalar.copy(plain[:], bank[:])
+            else:
+                nc.sync.dma_start(plain[:], window[:, :S])
 
         def stage_d(t):
             acc = psum.tile([P, S], F32, name="acc")
             product(acc[:], 1, t, gw[1][:], gs[1][:])
-            dc = work.tile([P, S], F32, name="dc")
+            dc = new("dc", 3)
             nc.scalar.copy(win_a[t][:, :S], acc[:])
-            nc.scalar.copy(dc[:], acc[:])
-            u = work.tile([P, S], F32, name="u")
-            nc.vector.tensor_tensor(u[:], win_a[t][:].indirect(l2[:]), dc[:], ALU.subtract)
-            g = keep.tile([P, S], F32, name="s1_%d" % t)
-            nc.scalar.activation(g[:], u[:], ACT.Sigmoid)
-            s1.append(g)
-
-        m1c = []
+            second_copy(dc, win_a[t], acc, t < 2)
+            u[t] = new("u", 3)
+            nc.vector.tensor_tensor(u[t][:], win_a[t][:].indirect(l2[:]), dc[:], ALU.subtract)
 
         def stage_y(t):
+            s1[t] = new("s1")
+            nc.scalar.activation(s1[t][:], u[t][:], ACT.Sigmoid)
             acc = psum.tile([P, S], F32, name="acc")
             product(acc[:], 0, t, gw[0][:], gs[0][:])
             nc.scalar.activation(win_y[t][:, :S], acc[:], ACT.Copy, scale=gain[:, t : t + 1])
-            near = work.tile([P, S], F32, name="near")
-            nc.vector.scalar_tensor_tensor(near[:], s1[t][:], 1.0, win_y[t][:, :S], ALU.subtract, ALU.mult)
-            far = work.tile([P, S], F32, name="far")
-            nc.vector.tensor_tensor(far[:], win_y[t][:].indirect(l1[:]), s1[t][:], ALU.mult)
-            nc.vector.tensor_tensor(win_a[t][:, :S], far[:], near[:], ALU.subtract)
-            c = work.tile([P, S], F32, name="m1c")
-            nc.scalar.copy(c[:], win_a[t][:, :S])
-            m1c.append(c)
+            far[t] = new("far", 4)
+            nc.vector.tensor_tensor(far[t][:], win_y[t][:].indirect(l1[:]), s1[t][:], ALU.mult)
+            near[t] = new("near", 4)
+            nc.vector.scalar_tensor_tensor(near[t][:], s1[t][:], -1.0 if t < NPE else 1.0, win_y[t][:, :S], ALU.mult if t < NPE else ALU.subtract, ALU.mult)
+
+        def stage_m1(t):
+            m1t[t] = new("m1t")
+            nc.scalar.copy(m1t[t][:], turned_sum([near[t], far[t], win_y[t]])[:])
+
+        def stage_m2(t):
+            m1c[t] = new("m1c", 3)
+            back = turned_sum([m1t[t]])
+            nc.scalar.copy(win_a[t][:, :S], back[:])
+            second_copy(m1c[t], win_a[t], back, t < NM)
+
+        def stage_mv(t):
+            m1c[t] = new("m1c", 3)
+            nc.vector.tensor_tensor(win_a[t][:, :S], far[t][:], near[t][:], ALU.subtract)
+            nc.scalar.copy(m1c[t][:], win_a[t][:, :S])
 
         def stage_b(t):
             acc = psum.tile([P, S], F32, name="acc")
             product(acc[:], 2, t, gw[2][:], gs[2][:])
-            bc = work.tile([P, S], F32, name="bc")
+            bc[t] = new("bc", 3)
             nc.scalar.copy(win_b[t][:, :S], acc[:])
-            nc.scalar.copy(bc[:], acc[:])
-            v = work.tile([P, S], F32, name="v")
-            nc.vector.tensor_tensor(v[:], win_b[t][:].indirect(l4[:]), bc[:], ALU.add)
-            nc.scalar.activation(s2_all[:, t, :], v[:], ACT.Sigmoid)
+            second_copy(bc[t], win_b[t], acc, t < NB)
+            v[t] = new("u", 3)
+            nc.vector.tensor_tensor(v[t][:], win_b[t][:].indirect(l4[:]), bc[t][:], ALU.add)
+
+        def gate2(t):
+            s2[t] = new("s2", 4)
+            nc.scalar.activation(s2[t][:], v[t][:], ACT.Sigmoid)
 
         def stage_p(t):
-            nc.vector.tensor_tensor(p_all[:, t, :], win_a[t][:].indirect(l3[:]), m1c[t][:], ALU.add)
+            pair[t] = new("pair", 2)
+            nc.vector.tensor_tensor(pair[t][:], win_a[t][:].indirect(l3[:]), m1c[t][:], ALU.add)
+
+        def stage_z(t, c0=0, c1=S):
+            nc.vector.tensor_tensor(z_rows[:, t, c0:c1], pair[t][:, c0:c1], s2[t][:, c0:c1], ALU.mult)
+
+        def weave(copy, t0, c0=0, c1=S):
+            copy(
+                zb[:].rearrange("p (c t) -> p c t", t=PACK)[:, c0:c1, t0 : t0 + 2],
+                z_rows[:, t0 : t0 + 2, c0:c1].rearrange("p t c -> p c t"),
+            )
 
         stage_d(0)
-        cast_w(0)
-        quant_w(0)
-        gather_words(2, l_three)
         stage_d(1)
         stage_d(2)
         stage_y(0)
         stage_d(3)
-        cast_w(2)
-        quant_w(2)
         stage_y(1)
-        stage_p(0)
-        stage_b(0)
+        cast_w(2, nc.scalar.copy, nc.scalar.copy)
+        quant_w(2)
         stage_y(2)
-        stage_p(1)
-        stage_b(1)
-        cast_w(3)
+        stage_m1(0)
         stage_y(3)
-        stage_p(2)
+        stage_b(0)
+        stage_b(1)
+        stage_m2(0)
         stage_b(2)
-        quant_w(3, 0, P)
+        stage_m1(1)
         stage_b(3)
+        stage_mv(3)
+        gate2(0)
+        stage_m2(1)
+        stage_m1(2)
+        stage_p(0)
+        gate2(1)
+        stage_m2(2)
+        gate2(2)
+        stage_p(1)
+        stage_z(0)
+        gate2(3)
+        nc.scalar.activation(warm2[:], s2[PACK - 1][:, 0:1], ACT.Abs_reciprocal_sqrt)
+        stage_p(2)
+        stage_z(1)
+        cast_w(3, nc.scalar.copy, nc.scalar.copy)
+        weave(nc.scalar.copy, 0)
+        quant_w(3, 0, P)
         stage_p(3)
-        nc.scalar.activation(warm2[:], s2_all[:, PACK - 1, 0:1], ACT.Abs_reciprocal_sqrt)
+        stage_z(2)
+        for c0 in (0, HALF):
+            stage_z(3, c0, c0 + HALF)
+        chunks = ((0, HALF), (HALF, HALF + P), (HALF + P, S))
+        def quant_z(c0, c1):
+            nc.vector.quantize_mx(zc[:, c0:c1].bitcast(FP8X4), zs[:, c0:c1], zb[:, PACK * c0 : PACK * c1])
 
-        for c0 in (0, HALF):
-            nc.vector.tensor_tensor(
-                zb[:, PACK * c0 : PACK * (c0 + HALF)].rearrange("p (c i t) -> p c t i", i=4, t=PACK),
-                p_all[:, :, c0 : c0 + HALF].rearrange("p t (c i) -> p c t i", i=4),
-                s2_all[:, :, c0 : c0 + HALF].rearrange("p t (c i) -> p c t i", i=4),
-                ALU.mult,
-            )
-        for c0 in (0, HALF):
-            nc.vector.quantize_mx(zc[:, c0 : c0 + HALF].bitcast(FP8X4), zs[:, c0 : c0 + HALF], zb[:, PACK * c0 : PACK * (c0 + HALF)])
+        weave(nc.vector.tensor_copy, 2, *chunks[0])
+        weave(nc.vector.tensor_copy, 2, *chunks[1])
+        quant_z(*chunks[0])
+        weave(nc.vector.tensor_copy, 2, *chunks[2])
+        quant_z(*chunks[1])
+        quant_z(*chunks[2])
+        late = keep.tile([P, S], U32, name="zb", align_bytes=64)
         for t in range(1, PACK):
-            quant_w(3, P * t, P * (t + 1))
+            nc.vector.quantize_mx(late[:, P * t : P * (t + 1)].bitcast(FP8X4), ws[3][:, P * t : P * (t + 1)], wb[3][:, S * t : S * (t + 1)])
 
         rows = out.rearrange("(p t) s -> p t s", t=PACK)
-        for t in range(PACK):
-            acc = psum.tile([P, S], F32, name="acc")
-            for c0 in (0, HALF):
-                product(acc[:, c0 : c0 + HALF], 3, t, zc[:, c0 : c0 + HALF], zs[:, c0 : c0 + HALF])
-            nc.scalar.copy(win_b[t][:, :S], acc[:])
-
-        held = []
-
-        def head(t):
-            h = win_b[t]
-            pa = work.tile([P, S], F32, name="pa")
-            nc.vector.tensor_copy(pa[:], h[:].indirect(l5[:]))
-            both = work.tile([P, S], F32, name="both")
-            nc.vector.tensor_tensor(both[:], h[:].indirect(l6[:]), pa[:], ALU.add)
-            diff = work.tile([P, S], F32, name="diff")
-            nc.vector.scalar_tensor_tensor(diff[:], pa[:], 2.0, both[:], ALU.mult, ALU.subtract)
-            mid = work.tile([P, S], F32, name="mid")
-            nc.vector.scalar_tensor_tensor(mid[:], h[:, :S], -5.0 / 3.0, both[:], ALU.mult, ALU.add)
-            num = work.tile([P, S], F32, name="num")
-            nc.vector.scalar_tensor_tensor(num[:], h[:, :S], 11.0 / 5.0, both[:], ALU.mult, ALU.subtract)
-            sq_d = work.tile([P, S], F32, name="sq_d")
-            nc.scalar.activation(sq_d[:], diff[:], ACT.Square, scale=math.sqrt(0.5))
-            sq_m = work.tile([P, S], F32, name="sq_m")
-            nc.scalar.activation(sq_m[:], mid[:], ACT.Square, scale=3.0 / 16.0 * math.sqrt(2.0))
-            held.append((num, sq_d, sq_m))
-
-        def tail(t):
-            num, sq_d, sq_m = held[t]
-            q = work.tile([P, S], F32, name="q")
-            nc.vector.tensor_tensor(q[:], sq_d[:], sq_m[:], ALU.add)
-            r = work.tile([P, S], F32, name="r")
-            nc.scalar.activation(r[:], q[:], ACT.Abs_reciprocal_sqrt, bias=quarter[:])
-            res = work.tile([P, S], F32, name="res")
-            nc.vector.scalar_tensor_tensor(res[:], num[:], 0.3125, r[:], ALU.mult, ALU.mult)
-            nc.sync.dma_start(rows[:, t, :], res[:])
-
-        head(0)
+        h0 = []
+        for c0, c1 in chunks:
+            acc = psum.tile([P, c1 - c0], F32, name="turned")
+            product(acc[:], 3, 0, zc[:, c0:c1], zs[:, c0:c1])
+            h0.append(acc)
+        h_acc = [None]
         for t in range(1, PACK):
-            head(t)
-            tail(t - 1)
-        tail(PACK - 1)
+            acc = psum.tile([P, S], F32, name="acc")
+            cols = slice(P * t, P * (t + 1))
+            nc.tensor.matmul_mx(
+                out=acc[:], lhsT=late[:, cols].bitcast(FP8X4), lhsT_scale=ws[3][:, cols],
+                rhs=zc[:].bitcast(FP8X4), rhs_scale=zs[:], start=True, stop=True,
+            )
+            h_acc.append(acc)
+
+        SC_D = math.sqrt(0.5)
+        SC_M = 3.0 / 16.0 * math.sqrt(2.0)
+        less, extra, first, second, num, root = {}, {}, {}, {}, {}, {}
+
+        def h_parts(t):
+            if t == 0:
+                return [(slice(c0, c1), acc[:]) for (c0, c1), acc in zip(chunks, h0)]
+            return [(slice(0, S), h_acc[t][:])]
+
+        def leave(t):
+            less[t] = new("less", 2)
+            for cols, acc in h_parts(t):
+                nc.scalar.copy(win_y[t][:, cols], acc)
+                nc.scalar.activation(less[t][:, cols], acc, ACT.Copy, scale=-11.0 / 5.0)
+
+        def leave_extra(t):
+            extra[t] = new("dc", 3) if t < 2 else new("once", 1)
+            nc.scalar.activation(extra[t][:], win_y[t][:, :S], ACT.Copy, scale=8.0 / 15.0)
+
+        def fetch1(t):
+            first[t] = new("first", 2)
+            nc.vector.tensor_tensor(first[t][:], win_y[t][:].indirect(l5[:]), less[t][:], ALU.add)
+
+        def fetch2(t):
+            second[t] = new("second", 3)
+            nc.vector.tensor_tensor(second[t][:], win_y[t][:].indirect(l6[:]), first[t][:], ALU.subtract)
+
+        def numer(t):
+            num[t] = new("num", 4)
+            nc.vector.scalar_tensor_tensor(num[t][:], first[t][:], 2.0, second[t][:], ALU.mult, ALU.add)
+
+        sq_d, sq_m, res_ = {}, {}, {}
+
+        def spread_d(t):
+            sq_d[t] = new("sq_d")
+            nc.scalar.activation(sq_d[t][:], turned_sum([second[t], less[t]])[:], ACT.Square, scale=SC_D)
+
+        def spread_m(t):
+            sq_m[t] = new("sq_m")
+            nc.scalar.activation(sq_m[t][:], turned_sum([num[t], extra[t]])[:], ACT.Square, scale=SC_M)
+
+        def spread_q(t):
+            root[t] = new("root", 3)
+            nc.scalar.activation(root[t][:], turned_sum([sq_m[t], sq_d[t]])[:], ACT.Abs_reciprocal_sqrt, bias=quarter[:])
+
+        def finish(t, c0=0, c1=S):
+            if t not in res_:
+                res_[t] = new("far", 4)
+            res = res_[t]
+            nc.vector.scalar_tensor_tensor(res[:, c0:c1], num[t][:, c0:c1], -0.3125, root[t][:, c0:c1], ALU.mult, ALU.mult)
+            nc.sync.dma_start(rows[:, t, c0:c1], res[:, c0:c1])
+
+        h = win_y[last]
+        leave(0)
+        fetch1(0)
+        leave_extra(0)
+        fetch2(0)
+        numer(0)
+        leave(1)
+        leave(2)
+        fetch1(1)
+        leave_extra(1)
+        spread_d(0)
+        fetch2(1)
+        leave_extra(2)
+        spread_m(0)
+        numer(1)
+        nc.scalar.copy(h[:, :S], h_acc[last][:])
+        fetch1(2)
+        spread_d(1)
+        fetch2(2)
+        spread_q(0)
+        numer(2)
+        spread_m(1)
+        pa = new("first", 2)
+        nc.vector.tensor_copy(pa[:], h[:].indirect(l5[:]))
+        spread_d(2)
+        spread_q(1)
+        both = new("second", 3)
+        nc.vector.tensor_tensor(both[:], h[:].indirect(l6[:]), pa[:], ALU.add)
+        spread_m(2)
+        finish(0)
+        diff, mid = new("diff", 1), new("mid", 1)
+        nc.vector.scalar_tensor_tensor(diff[:], pa[:], 2.0, both[:], ALU.mult, ALU.subtract)
+        nc.vector.scalar_tensor_tensor(mid[:], h[:, :S], -5.0 / 3.0, both[:], ALU.mult, ALU.add)
+        num[last] = new("num", 4)
+        nc.vector.scalar_tensor_tensor(num[last][:], h[:, :S], -11.0 / 5.0, both[:], ALU.mult, ALU.add)
+        sq_d3, sq_m3 = new("sq_d"), new("once", 1)
+        nc.scalar.activation(sq_d3[:], diff[:], ACT.Square, scale=SC_D)
+        nc.scalar.activation(sq_m3[:], mid[:], ACT.Square, scale=SC_M)
+        spread_q(2)
+        finish(1)
+        q = new("diff", 1)
+        root[last] = new("root", 3)
+        for c0 in (0, HALF):
+            nc.vector.tensor_tensor(q[:, c0 : c0 + HALF], sq_d3[:, c0 : c0 + HALF], sq_m3[:, c0 : c0 + HALF], ALU.add)
+            nc.scalar.activation(root[last][:, c0 : c0 + HALF], q[:, c0 : c0 + HALF], ACT.Abs_reciprocal_sqrt, bias=quarter[:])
+        finish(2)
+        for c0 in (0, HALF):
+            finish(last, c0, c0 + HALF)

@@ -43,12 +43,13 @@ def tile_picked_triopullbtriebstd_none_p_kernel(tc, x_words, x_scales, w1, w2, w
         quarter = keep.tile([P, 1], F32, name="quarter")
         warm = keep.tile([P, 1], F32, name="warm")
         warm2 = keep.tile([P, 1], F32, name="warm2")
-        raw = [[keep.tile([P, PACK, HALF], F32, name="raw%d_%d" % (i, a)) for a in range(2)] for i in range(4)]
+        whole = [keep.tile([P, PACK, S], F32, name="raw%d" % i) for i in range(4)]
+        raw = [[whole[i][:, :, a * HALF : (a + 1) * HALF] for a in range(2)] for i in range(4)]
         ident = keep.tile([P, P], F32, name="ident")
-        wb = [keep.tile([P, PACK * S], BF16, name="wb%d" % i, align_bytes=64) for i in range(4)]
-        wc = [keep.tile([P, S], U32, name="wc%d" % i, align_bytes=64) for i in range(4)]
+        wb = [keep.tile([P, PACK * S], BF16, name="wb%d" % i, align_bytes=64) for i in range(3)]
+        wc = {i: keep.tile([P, S], U32, name="wc%d" % i, align_bytes=64) for i in range(4)}
         ws = [keep.tile([P, S], U8, name="ws%d" % i, align_bytes=64) for i in range(4)]
-        gw = [keep.tile([P, S], U32, name="gw%d" % i, align_bytes=64) for i in range(2)]
+        gw = [keep.tile([P, S], U32, name="gw%d" % i, align_bytes=64) for i in range(3)]
         win_b = [keep.tile([P, WIN], F32, name="wb_%d" % t) for t in range(PACK)]
         gs = [keep.tile([P, S], U8, name="gs%d" % i, align_bytes=64) for i in range(3)]
         win_a = [keep.tile([P, WIN], F32, name="wa%d" % t) for t in range(PACK)]
@@ -58,19 +59,18 @@ def tile_picked_triopullbtriebstd_none_p_kernel(tc, x_words, x_scales, w1, w2, w
         zc = keep.tile([P, S], U32, name="zc", align_bytes=64)
         zs = keep.tile([P, S], U8, name="zs", align_bytes=64)
 
-        for q in range(4):
-            rows4 = x_scales[0, 4 * q : 4 * q + 4, :].bitcast(I32).rearrange("r c -> (r c)")
-            nc.sync.dma_start(xs[32 * q : 32 * (q + 1), :].bitcast(I32), rows4.partition_broadcast(8))
+        nc.gpsimd.memset(xs[:].bitcast(I32), 0)
         nc.sync.dma_start(l_two[:], two)
         nc.sync.dma_start(l_offs[:], offs)
+        for q in range(4):
+            nc.sync.dma_start(xs[32 * q : 32 * q + 4, :].bitcast(I32), x_scales[0, 4 * q : 4 * q + 4, :].bitcast(I32))
         nc.sync.dma_start(l_three[:], three)
-        nc.sync.dma_start(xw[:].bitcast(I32), x_words[0].rearrange("p n t -> p (n t)").bitcast(I32))
 
         def load_w(i, w):
-            for a in range(2):
-                nc.sync.dma_start(raw[i][a][:], w.rearrange("(p j) c -> p j c", j=PACK)[:, :, a * HALF : (a + 1) * HALF])
+            nc.sync.dma_start(whole[i][:], w.rearrange("(p j) c -> p j c", j=PACK))
 
         load_w(1, w2)
+        nc.sync.dma_start(xw[:].bitcast(I32), x_words[0].rearrange("p n t -> p (n t)").bitcast(I32))
         load_w(0, w1)
         nc.sync.dma_start(l2[:], n2)
         nc.sync.dma_start(gain[:], gn.rearrange("(p t) o -> p (t o)", t=PACK))
@@ -123,13 +123,12 @@ def tile_picked_triopullbtriebstd_none_p_kernel(tc, x_words, x_scales, w1, w2, w
         gather_bytes(1, l_two)
         gather_bytes(0, l_offs)
         gather_bytes(2, l_three)
+        cast_w(1, nc.scalar.copy, nc.vector.tensor_copy)
+        quant_w(1)
         gather_words(1, l_two)
         gather_words(0, l_offs)
-        cast_w(1, nc.scalar.copy, nc.scalar.copy)
-        quant_w(1)
-        gw.append(keep.tile([P, S], U32, name="wb1", align_bytes=64))
         gather_words(2, l_three)
-        cast_w(0, nc.scalar.copy, nc.vector.tensor_copy)
+        cast_w(0, nc.vector.tensor_copy, nc.vector.tensor_copy)
         quant_w(0)
 
         def turned_sum(parts, name="turned"):
@@ -147,7 +146,7 @@ def tile_picked_triopullbtriebstd_none_p_kernel(tc, x_words, x_scales, w1, w2, w
         s1, s2, m1c, near, far, pair = {}, {}, {}, {}, {}, {}
 
         u, v, bc, m1t, dc_, = {}, {}, {}, {}, {}
-        NM, NB = 3, 1
+        NM, NB = 2, 0
 
         def second_copy(plain, window, bank, soon):
             if soon:
@@ -160,17 +159,17 @@ def tile_picked_triopullbtriebstd_none_p_kernel(tc, x_words, x_scales, w1, w2, w
             product(acc[:], 1, t, gw[1][:], gs[1][:])
             dc = new("dc", 3)
             nc.scalar.copy(win_a[t][:, :S], acc[:])
-            second_copy(dc, win_a[t], acc, t < 2)
-            u[t] = new("u", 3)
+            second_copy(dc, win_a[t], acc, True)
+            u[t] = new("u", 4)
             nc.vector.tensor_tensor(u[t][:], win_a[t][:].indirect(l2[:]), dc[:], ALU.subtract)
 
         def stage_y(t):
-            s1[t] = new("s1")
+            s1[t] = new("s1", 4)
             nc.scalar.activation(s1[t][:], u[t][:], ACT.Sigmoid)
             acc = psum.tile([P, S], F32, name="acc")
             product(acc[:], 0, t, gw[0][:], gs[0][:])
             nc.scalar.activation(win_y[t][:, :S], acc[:], ACT.Copy, scale=gain[:, t : t + 1])
-            far[t] = new("far", 4)
+            far[t] = new("far", 4) if t < last else keep.tile([P, S], F32, name="wb3", align_bytes=64)
             nc.vector.tensor_tensor(far[t][:], win_y[t][:].indirect(l1[:]), s1[t][:], ALU.mult)
             near[t] = new("near", 4)
             nc.vector.scalar_tensor_tensor(near[t][:], s1[t][:], -1.0 if t < NPE else 1.0, win_y[t][:, :S], ALU.mult if t < NPE else ALU.subtract, ALU.mult)
@@ -183,7 +182,7 @@ def tile_picked_triopullbtriebstd_none_p_kernel(tc, x_words, x_scales, w1, w2, w
             m1c[t] = new("m1c", 3)
             back = turned_sum([m1t[t]])
             nc.scalar.copy(win_a[t][:, :S], back[:])
-            second_copy(m1c[t], win_a[t], back, t < NM)
+            second_copy(m1c[t], win_a[t], back, t != 1)
 
         def stage_mv(t):
             m1c[t] = new("m1c", 3)
@@ -195,12 +194,12 @@ def tile_picked_triopullbtriebstd_none_p_kernel(tc, x_words, x_scales, w1, w2, w
             product(acc[:], 2, t, gw[2][:], gs[2][:])
             bc[t] = new("bc", 3)
             nc.scalar.copy(win_b[t][:, :S], acc[:])
-            second_copy(bc[t], win_b[t], acc, t < NB)
-            v[t] = new("u", 3)
+            second_copy(bc[t], win_b[t], acc, t < 1)
+            v[t] = new("u", 4)
             nc.vector.tensor_tensor(v[t][:], win_b[t][:].indirect(l4[:]), bc[t][:], ALU.add)
 
         def gate2(t):
-            s2[t] = new("s2", 4)
+            s2[t] = new("s1", 4)
             nc.scalar.activation(s2[t][:], v[t][:], ACT.Sigmoid)
 
         def stage_p(t):
@@ -219,14 +218,14 @@ def tile_picked_triopullbtriebstd_none_p_kernel(tc, x_words, x_scales, w1, w2, w
         stage_d(0)
         stage_d(1)
         stage_d(2)
-        stage_y(0)
         stage_d(3)
+        stage_y(0)
         stage_y(1)
         cast_w(2, nc.scalar.copy, nc.scalar.copy)
         quant_w(2)
         stage_y(2)
-        stage_m1(0)
         stage_y(3)
+        stage_m1(0)
         stage_b(0)
         stage_b(1)
         stage_m2(0)
@@ -234,9 +233,9 @@ def tile_picked_triopullbtriebstd_none_p_kernel(tc, x_words, x_scales, w1, w2, w
         stage_m1(1)
         stage_b(3)
         stage_mv(3)
-        gate2(0)
         stage_m2(1)
         stage_m1(2)
+        gate2(0)
         stage_p(0)
         gate2(1)
         stage_m2(2)
@@ -247,6 +246,7 @@ def tile_picked_triopullbtriebstd_none_p_kernel(tc, x_words, x_scales, w1, w2, w
         nc.scalar.activation(warm2[:], s2[PACK - 1][:, 0:1], ACT.Abs_reciprocal_sqrt)
         stage_p(2)
         stage_z(1)
+        wb.append(keep.tile([P, PACK * S], BF16, name="wb3", align_bytes=64))
         cast_w(3, nc.scalar.copy, nc.scalar.copy)
         weave(nc.scalar.copy, 0)
         quant_w(3, 0, P)
@@ -258,7 +258,7 @@ def tile_picked_triopullbtriebstd_none_p_kernel(tc, x_words, x_scales, w1, w2, w
         def quant_z(c0, c1):
             nc.vector.quantize_mx(zc[:, c0:c1].bitcast(FP8X4), zs[:, c0:c1], zb[:, PACK * c0 : PACK * c1])
 
-        weave(nc.vector.tensor_copy, 2, *chunks[0])
+        weave(nc.scalar.copy, 2, *chunks[0])
         weave(nc.vector.tensor_copy, 2, *chunks[1])
         quant_z(*chunks[0])
         weave(nc.vector.tensor_copy, 2, *chunks[2])
@@ -294,7 +294,7 @@ def tile_picked_triopullbtriebstd_none_p_kernel(tc, x_words, x_scales, w1, w2, w
             return [(slice(0, S), h_acc[t][:])]
 
         def leave(t):
-            less[t] = new("less", 2)
+            less[t] = new("less", 3)
             for cols, acc in h_parts(t):
                 nc.scalar.copy(win_y[t][:, cols], acc)
                 nc.scalar.activation(less[t][:, cols], acc, ACT.Copy, scale=-11.0 / 5.0)
@@ -339,31 +339,31 @@ def tile_picked_triopullbtriebstd_none_p_kernel(tc, x_words, x_scales, w1, w2, w
         h = win_y[last]
         leave(0)
         fetch1(0)
-        leave_extra(0)
-        fetch2(0)
-        numer(0)
         leave(1)
-        leave(2)
+        fetch2(0)
         fetch1(1)
-        leave_extra(1)
+        leave_extra(0)
+        numer(0)
+        leave(2)
         spread_d(0)
         fetch2(1)
-        leave_extra(2)
+        leave_extra(1)
+        fetch1(2)
         spread_m(0)
         numer(1)
         nc.scalar.copy(h[:, :S], h_acc[last][:])
-        fetch1(2)
+        leave_extra(2)
         spread_d(1)
         fetch2(2)
         spread_q(0)
-        numer(2)
-        spread_m(1)
         pa = new("first", 2)
         nc.vector.tensor_copy(pa[:], h[:].indirect(l5[:]))
+        numer(2)
+        spread_m(1)
         spread_d(2)
-        spread_q(1)
         both = new("second", 3)
         nc.vector.tensor_tensor(both[:], h[:].indirect(l6[:]), pa[:], ALU.add)
+        spread_q(1)
         spread_m(2)
         finish(0)
         diff, mid = new("diff", 1), new("mid", 1)
@@ -381,6 +381,7 @@ def tile_picked_triopullbtriebstd_none_p_kernel(tc, x_words, x_scales, w1, w2, w
         for c0 in (0, HALF):
             nc.vector.tensor_tensor(q[:, c0 : c0 + HALF], sq_d3[:, c0 : c0 + HALF], sq_m3[:, c0 : c0 + HALF], ALU.add)
             nc.scalar.activation(root[last][:, c0 : c0 + HALF], q[:, c0 : c0 + HALF], ACT.Abs_reciprocal_sqrt, bias=quarter[:])
-        finish(2)
+        for c0 in (0, HALF):
+            finish(2, c0, c0 + HALF)
         for c0 in (0, HALF):
             finish(last, c0, c0 + HALF)

@@ -336,7 +336,42 @@ def tile_picked_triopullbtriebstd_none_p_kernel(tc, x_words, x_scales, w1, w2, w
             nc.vector.scalar_tensor_tensor(res[:, c0:c1], num[t][:, c0:c1], -0.3125, root[t][:, c0:c1], ALU.mult, ALU.mult)
             nc.sync.dma_start(rows[:, t, c0:c1], res[:, c0:c1])
 
-        h = win_y[last]
+        both, pa = {}, {}
+
+        def leave_plain(t):
+            nc.scalar.copy(win_y[t][:, :S], h_acc[t][:])
+
+        def fetch_a(t):
+            pa[t] = new("first", 2)
+            nc.vector.tensor_copy(pa[t][:], win_y[t][:].indirect(l5[:]))
+
+        def fetch_both(t):
+            both[t] = new("second", 3)
+            nc.vector.tensor_tensor(both[t][:], win_y[t][:].indirect(l6[:]), pa[t][:], ALU.add)
+
+        def plain_d(t):
+            diff = new("diff")
+            nc.vector.scalar_tensor_tensor(diff[:], pa[t][:], 2.0, both[t][:], ALU.mult, ALU.subtract)
+            sq_d[t] = new("dc", 3)
+            nc.scalar.activation(sq_d[t][:], diff[:], ACT.Square, scale=SC_D)
+
+        def plain_m(t):
+            mid = new("diff")
+            nc.vector.scalar_tensor_tensor(mid[:], win_y[t][:, :S], -5.0 / 3.0, both[t][:], ALU.mult, ALU.add)
+            sq_m[t] = new("dc", 3) if t < last else new("less", 3)
+            nc.scalar.activation(sq_m[t][:], mid[:], ACT.Square, scale=SC_M)
+
+        def plain_n(t):
+            num[t] = new("num", 4)
+            nc.vector.scalar_tensor_tensor(num[t][:], win_y[t][:, :S], -11.0 / 5.0, both[t][:], ALU.mult, ALU.add)
+
+        def plain_q(t, pieces):
+            q = new("m1c", 3)
+            root[t] = new("root", 3)
+            for c0, c1 in pieces:
+                nc.vector.tensor_tensor(q[:, c0:c1], sq_d[t][:, c0:c1], sq_m[t][:, c0:c1], ALU.add)
+                nc.scalar.activation(root[t][:, c0:c1], q[:, c0:c1], ACT.Abs_reciprocal_sqrt, bias=quarter[:])
+
         leave(0)
         fetch1(0)
         leave(1)
@@ -344,44 +379,31 @@ def tile_picked_triopullbtriebstd_none_p_kernel(tc, x_words, x_scales, w1, w2, w
         fetch1(1)
         leave_extra(0)
         numer(0)
-        leave(2)
+        leave_plain(2)
         spread_d(0)
         fetch2(1)
         leave_extra(1)
-        fetch1(2)
+        fetch_a(2)
         spread_m(0)
         numer(1)
-        nc.scalar.copy(h[:, :S], h_acc[last][:])
-        leave_extra(2)
+        leave_plain(3)
         spread_d(1)
-        fetch2(2)
+        fetch_both(2)
+        fetch_a(3)
         spread_q(0)
-        pa = new("first", 2)
-        nc.vector.tensor_copy(pa[:], h[:].indirect(l5[:]))
-        numer(2)
+        plain_d(2)
+        plain_m(2)
         spread_m(1)
-        spread_d(2)
-        both = new("second", 3)
-        nc.vector.tensor_tensor(both[:], h[:].indirect(l6[:]), pa[:], ALU.add)
+        fetch_both(3)
+        plain_n(2)
         spread_q(1)
-        spread_m(2)
+        plain_d(3)
+        plain_m(3)
+        plain_q(2, [(0, S)])
         finish(0)
-        diff, mid = new("diff", 1), new("mid", 1)
-        nc.vector.scalar_tensor_tensor(diff[:], pa[:], 2.0, both[:], ALU.mult, ALU.subtract)
-        nc.vector.scalar_tensor_tensor(mid[:], h[:, :S], -5.0 / 3.0, both[:], ALU.mult, ALU.add)
-        num[last] = new("num", 4)
-        nc.vector.scalar_tensor_tensor(num[last][:], h[:, :S], -11.0 / 5.0, both[:], ALU.mult, ALU.add)
-        sq_d3, sq_m3 = new("sq_d"), new("once", 1)
-        nc.scalar.activation(sq_d3[:], diff[:], ACT.Square, scale=SC_D)
-        nc.scalar.activation(sq_m3[:], mid[:], ACT.Square, scale=SC_M)
-        spread_q(2)
+        plain_n(3)
         finish(1)
-        q = new("diff", 1)
-        root[last] = new("root", 3)
-        for c0 in (0, HALF):
-            nc.vector.tensor_tensor(q[:, c0 : c0 + HALF], sq_d3[:, c0 : c0 + HALF], sq_m3[:, c0 : c0 + HALF], ALU.add)
-            nc.scalar.activation(root[last][:, c0 : c0 + HALF], q[:, c0 : c0 + HALF], ACT.Abs_reciprocal_sqrt, bias=quarter[:])
-        for c0 in (0, HALF):
-            finish(2, c0, c0 + HALF)
+        plain_q(3, [(0, HALF), (HALF, S)])
+        finish(2)
         for c0 in (0, HALF):
             finish(last, c0, c0 + HALF)

import math
from contextlib import ExitStack

import concourse.mybir as mybir
from concourse.masks import make_identity

F32 = mybir.dt.float32
BF16 = mybir.dt.bfloat16
I32 = mybir.dt.int32
U32 = mybir.dt.uint32
U16 = mybir.dt.uint16
U8 = mybir.dt.uint8
FP8X4 = mybir.dt.float8_e4m3fn_x4
ACT = mybir.ActivationFunctionType
ALU = mybir.AluOpType

P = 128
PACK = 4
T = 2048
S = 512
WIN = 2 * S
HALF = S // 2
FLOPS = 4 * 2 * 512 * 512 * 512


def tile_picked_triopullbtriebstd_none_p_kernel(tc, x_words, x_scales, w1, w2, w3, gn, w4, offs, two, three, n1, n2, n3, n4, n5, n6, out):
    nc = tc.nc
    with ExitStack() as ctx:
        keep = ctx.enter_context(tc.tile_pool(name="keep", bufs=1))
        work = ctx.enter_context(tc.tile_pool(name="work", bufs=2))
        psum = ctx.enter_context(tc.psum_pool(name="psum", bufs=4))

        def list_tile(name):
            return keep.tile([P, S // 16], U16, name=name)

        l_offs, l_two, l_three = list_tile("l_offs"), list_tile("l_two"), list_tile("l_three")
        l1, l2, l3 = list_tile("l1"), list_tile("l2"), list_tile("l3")
        l4, l5, l6 = list_tile("l4"), list_tile("l5"), list_tile("l6")

        xw = keep.tile([P, T], U32, name="xw", align_bytes=64)
        xs = keep.tile([P, T], U8, name="xs", align_bytes=64)
        gain = keep.tile([P, PACK], F32, name="gain")
        quarter = keep.tile([P, 1], F32, name="quarter")
        warm = keep.tile([P, 1], F32, name="warm")
        warm2 = keep.tile([P, 1], F32, name="warm2")
        whole = [keep.tile([P, PACK, S], F32, name="raw%d" % i) for i in range(4)]
        raw = [[whole[i][:, :, a * HALF : (a + 1) * HALF] for a in range(2)] for i in range(4)]
        ident = keep.tile([P, P], F32, name="ident")
        wb = [keep.tile([P, PACK * S], BF16, name="wb%d" % i, align_bytes=64) for i in range(3)]
        wc = {i: keep.tile([P, S], U32, name="wc%d" % i, align_bytes=64) for i in range(4)}
        ws = [keep.tile([P, S], U8, name="ws%d" % i, align_bytes=64) for i in range(4)]
        gw = [keep.tile([P, S], U32, name="gw%d" % i, align_bytes=64) for i in range(3)]
        win_b = [keep.tile([P, WIN], F32, name="wb_%d" % t) for t in range(PACK)]
        gs = [keep.tile([P, S], U8, name="gs%d" % i, align_bytes=64) for i in range(3)]
        win_a = [keep.tile([P, WIN], F32, name="wa%d" % t) for t in range(PACK)]
        win_y = [keep.tile([P, WIN], F32, name="wy%d" % t) for t in range(PACK)]
        z_rows = keep.tile([P, PACK, S], BF16, name="z_rows")
        zb = keep.tile([P, S * PACK], BF16, name="zb", align_bytes=64)
        zc = keep.tile([P, S], U32, name="zc", align_bytes=64)
        zs = keep.tile([P, S], U8, name="zs", align_bytes=64)

        nc.gpsimd.memset(xs[:].bitcast(I32), 0)
        nc.sync.dma_start(l_two[:], two)
        nc.sync.dma_start(l_offs[:], offs)
        for q in range(4):
            nc.sync.dma_start(xs[32 * q : 32 * q + 4, :].bitcast(I32), x_scales[0, 4 * q : 4 * q + 4, :].bitcast(I32))
        nc.sync.dma_start(l_three[:], three)

        def load_w(i, w):
            nc.sync.dma_start(whole[i][:], w.rearrange("(p j) c -> p j c", j=PACK))

        load_w(1, w2)
        nc.sync.dma_start(xw[:].bitcast(I32), x_words[0].rearrange("p n t -> p (n t)").bitcast(I32))
        load_w(0, w1)
        nc.sync.dma_start(l2[:], n2)
        nc.sync.dma_start(gain[:], gn.rearrange("(p t) o -> p (t o)", t=PACK))
        nc.sync.dma_start(l1[:], n1)
        load_w(2, w3)
        nc.sync.dma_start(l4[:], n4)
        nc.sync.dma_start(l3[:], n3)
        load_w(3, w4)
        nc.sync.dma_start(l5[:], n5)
        nc.sync.dma_start(l6[:], n6)

        nc.vector.memset(quarter[:], 0.25)
        nc.scalar.activation(warm[:], quarter[:], ACT.Sigmoid)
        for t in range(PACK):
            nc.gpsimd.memset(win_y[t][:, S:], 0.0)
        for t in range(PACK):
            nc.vector.memset(win_b[t][:, S:], 0.0)
        for t in range(PACK):
            nc.scalar.copy(win_a[t][:, S:], win_y[0][:, S:])
        make_identity(nc, ident[:])

        def cast_w(i, *copies):
            for a, copy in enumerate(copies):
                if copy is None:
                    continue
                copy(
                    wb[i][:].rearrange("p (t m j) -> p m t j", t=PACK, j=PACK)[:, a * P // 2 : (a + 1) * P // 2],
                    raw[i][a][:].rearrange("p j (m t) -> p m t j", t=PACK),
                )

        def quant_w(i, c0=0, c1=S):
            nc.vector.quantize_mx(wc[i][:, c0:c1].bitcast(FP8X4), ws[i][:, c0:c1], wb[i][:, PACK * c0 : PACK * c1])

        def product(acc, i, t, words, scales):
            cols = slice(P * t, P * (t + 1))
            nc.tensor.matmul_mx(
                out=acc, lhsT=wc[i][:, cols].bitcast(FP8X4), lhsT_scale=ws[i][:, cols],
                rhs=words.bitcast(FP8X4), rhs_scale=scales, start=True, stop=True,
            )

        def gather_bytes(i, lst):
            nc.vector.tensor_copy(gs[i][:], xs[:].indirect(lst[:]))

        def gather_words(i, lst):
            nc.vector.tensor_copy(gw[i][:], xw[:].indirect(lst[:]))

        def new(name, bufs=2):
            return work.tile([P, S], F32, name=name, bufs=bufs)

        gather_bytes(1, l_two)
        gather_bytes(0, l_offs)
        gather_bytes(2, l_three)
        cast_w(1, nc.scalar.copy, nc.vector.tensor_copy)
        quant_w(1)
        gather_words(1, l_two)
        gather_words(0, l_offs)
        gather_words(2, l_three)
        cast_w(0, nc.vector.tensor_copy, nc.vector.tensor_copy)
        quant_w(0)

        def turned_sum(parts, name="turned"):
            bank = psum.tile([P, S], F32, name=name)
            for c0 in range(0, S, P):
                for k, part in enumerate(parts):
                    nc.tensor.matmul(
                        bank[:, c0 : c0 + P], part[:, c0 : c0 + P], ident[:],
                        start=(k == 0), stop=(k == len(parts) - 1), is_transpose=True,
                    )
            return bank

        last = PACK - 1
        NPE = 3
        s1, s2, m1c, near, far, pair = {}, {}, {}, {}, {}, {}

        u, v, bc, m1t, dc_, = {}, {}, {}, {}, {}
        NM, NB = 2, 0

        def second_copy(plain, window, bank, soon):
            if soon:
                nc.scalar.copy(plain[:], bank[:])
            else:
                nc.sync.dma_start(plain[:], window[:, :S])

        def stage_d(t):
            acc = psum.tile([P, S], F32, name="acc")
            product(acc[:], 1, t, gw[1][:], gs[1][:])
            dc = new("dc", 3)
            nc.scalar.copy(win_a[t][:, :S], acc[:])
            second_copy(dc, win_a[t], acc, True)
            u[t] = new("u", 4)
            nc.vector.tensor_tensor(u[t][:], win_a[t][:].indirect(l2[:]), dc[:], ALU.subtract)

        def stage_y(t):
            s1[t] = new("s1", 4)
            nc.scalar.activation(s1[t][:], u[t][:], ACT.Sigmoid)
            acc = psum.tile([P, S], F32, name="acc")
            product(acc[:], 0, t, gw[0][:], gs[0][:])
            nc.scalar.activation(win_y[t][:, :S], acc[:], ACT.Copy, scale=gain[:, t : t + 1])
            far[t] = new("far", 4) if t < last else keep.tile([P, S], F32, name="wb3", align_bytes=64)
            nc.vector.tensor_tensor(far[t][:], win_y[t][:].indirect(l1[:]), s1[t][:], ALU.mult)
            near[t] = new("near", 4)
            nc.vector.scalar_tensor_tensor(near[t][:], s1[t][:], -1.0 if t < NPE else 1.0, win_y[t][:, :S], ALU.mult if t < NPE else ALU.subtract, ALU.mult)

        def stage_m1(t):
            m1t[t] = new("m1t")
            nc.scalar.copy(m1t[t][:], turned_sum([near[t], far[t], win_y[t]])[:])

        def stage_m2(t):
            m1c[t] = new("m1c", 3)
            back = turned_sum([m1t[t]])
            nc.scalar.copy(win_a[t][:, :S], back[:])
            second_copy(m1c[t], win_a[t], back, t != 1)

        def stage_mv(t):
            m1c[t] = new("m1c", 3)
            nc.vector.tensor_tensor(win_a[t][:, :S], far[t][:], near[t][:], ALU.subtract)
            nc.scalar.copy(m1c[t][:], win_a[t][:, :S])

        def stage_b(t):
            acc = psum.tile([P, S], F32, name="acc")
            product(acc[:], 2, t, gw[2][:], gs[2][:])
            bc[t] = new("bc", 3)
            nc.scalar.copy(win_b[t][:, :S], acc[:])
            second_copy(bc[t], win_b[t], acc, t < 1)
            v[t] = new("u", 4)
            nc.vector.tensor_tensor(v[t][:], win_b[t][:].indirect(l4[:]), bc[t][:], ALU.add)

        def gate2(t):
            s2[t] = new("s1", 4)
            nc.scalar.activation(s2[t][:], v[t][:], ACT.Sigmoid)

        def stage_p(t):
            pair[t] = new("pair", 2)
            nc.vector.tensor_tensor(pair[t][:], win_a[t][:].indirect(l3[:]), m1c[t][:], ALU.add)

        def stage_z(t, c0=0, c1=S):
            nc.vector.tensor_tensor(z_rows[:, t, c0:c1], pair[t][:, c0:c1], s2[t][:, c0:c1], ALU.mult)

        def weave(copy, t0, c0=0, c1=S):
            copy(
                zb[:].rearrange("p (c t) -> p c t", t=PACK)[:, c0:c1, t0 : t0 + 2],
                z_rows[:, t0 : t0 + 2, c0:c1].rearrange("p t c -> p c t"),
            )

        stage_d(0)
        stage_d(1)
        stage_d(2)
        stage_d(3)
        stage_y(0)
        stage_y(1)
        cast_w(2, nc.scalar.copy, nc.scalar.copy)
        quant_w(2)
        stage_y(2)
        stage_y(3)
        stage_m1(0)
        stage_b(0)
        stage_b(1)
        stage_m2(0)
        stage_b(2)
        stage_m1(1)
        stage_b(3)
        stage_mv(3)
        stage_m2(1)
        stage_m1(2)
        gate2(0)
        stage_p(0)
        gate2(1)
        stage_m2(2)
        gate2(2)
        stage_p(1)
        stage_z(0)
        gate2(3)
        nc.scalar.activation(warm2[:], s2[PACK - 1][:, 0:1], ACT.Abs_reciprocal_sqrt)
        stage_p(2)
        stage_z(1)
        wb.append(keep.tile([P, PACK * S], BF16, name="wb3", align_bytes=64))
        cast_w(3, nc.scalar.copy, nc.scalar.copy)
        weave(nc.scalar.copy, 0)
        quant_w(3, 0, P)
        stage_p(3)
        stage_z(2)
        for c0 in (0, HALF):
            stage_z(3, c0, c0 + HALF)
        chunks = ((0, HALF), (HALF, HALF + P), (HALF + P, S))
        def quant_z(c0, c1):
            nc.vector.quantize_mx(zc[:, c0:c1].bitcast(FP8X4), zs[:, c0:c1], zb[:, PACK * c0 : PACK * c1])

        weave(nc.scalar.copy, 2, *chunks[0])
        weave(nc.vector.tensor_copy, 2, *chunks[1])
        quant_z(*chunks[0])
        weave(nc.vector.tensor_copy, 2, *chunks[2])
        quant_z(*chunks[1])
        quant_z(*chunks[2])
        late = keep.tile([P, S], U32, name="zb", align_bytes=64)
        for t in range(1, PACK):
            nc.vector.quantize_mx(late[:, P * t : P * (t + 1)].bitcast(FP8X4), ws[3][:, P * t : P * (t + 1)], wb[3][:, S * t : S * (t + 1)])

        rows = out.rearrange("(p t) s -> p t s", t=PACK)
        h0 = []
        for c0, c1 in chunks:
            acc = psum.tile([P, c1 - c0], F32, name="turned")
            product(acc[:], 3, 0, zc[:, c0:c1], zs[:, c0:c1])
            h0.append(acc)
        h_acc = [None]
        for t in range(1, PACK):
            acc = psum.tile([P, S], F32, name="acc")
            cols = slice(P * t, P * (t + 1))
            nc.tensor.matmul_mx(
                out=acc[:], lhsT=late[:, cols].bitcast(FP8X4), lhsT_scale=ws[3][:, cols],
                rhs=zc[:].bitcast(FP8X4), rhs_scale=zs[:], start=True, stop=True,
            )
            h_acc.append(acc)

        SC_D = math.sqrt(0.5)
        SC_M = 3.0 / 16.0 * math.sqrt(2.0)
        less, extra, first, second, num, root = {}, {}, {}, {}, {}, {}

        def h_parts(t):
            if t == 0:
                return [(slice(c0, c1), acc[:]) for (c0, c1), acc in zip(chunks, h0)]
            return [(slice(0, S), h_acc[t][:])]

        def leave(t):
            less[t] = new("less", 3)
            for cols, acc in h_parts(t):
                nc.scalar.copy(win_y[t][:, cols], acc)
                nc.scalar.activation(less[t][:, cols], acc, ACT.Copy, scale=-11.0 / 5.0)

        def leave_extra(t):
            extra[t] = new("dc", 3) if t < 2 else new("once", 1)
            nc.scalar.activation(extra[t][:], win_y[t][:, :S], ACT.Copy, scale=8.0 / 15.0)

        def fetch1(t):
            first[t] = new("first", 2)
            nc.vector.tensor_tensor(first[t][:], win_y[t][:].indirect(l5[:]), less[t][:], ALU.add)

        def fetch2(t):
            second[t] = new("second", 3)
            nc.vector.tensor_tensor(second[t][:], win_y[t][:].indirect(l6[:]), first[t][:], ALU.subtract)

        def numer(t):
            num[t] = new("num", 4)
            nc.vector.scalar_tensor_tensor(num[t][:], first[t][:], 2.0, second[t][:], ALU.mult, ALU.add)

        sq_d, sq_m, res_ = {}, {}, {}

        def spread_d(t):
            sq_d[t] = new("sq_d")
            nc.scalar.activation(sq_d[t][:], turned_sum([second[t], less[t]])[:], ACT.Square, scale=SC_D)

        def spread_m(t):
            sq_m[t] = new("sq_m")
            nc.scalar.activation(sq_m[t][:], turned_sum([num[t], extra[t]])[:], ACT.Square, scale=SC_M)

        def spread_q(t):
            root[t] = new("root", 3)
            nc.scalar.activation(root[t][:], turned_sum([sq_m[t], sq_d[t]])[:], ACT.Abs_reciprocal_sqrt, bias=quarter[:])

        def finish(t, c0=0, c1=S):
            if t not in res_:
                res_[t] = new("far", 4)
            res = res_[t]
            nc.vector.scalar_tensor_tensor(res[:, c0:c1], num[t][:, c0:c1], -0.3125, root[t][:, c0:c1], ALU.mult, ALU.mult)
            nc.sync.dma_start(rows[:, t, c0:c1], res[:, c0:c1])

        both, pa = {}, {}

        def leave_plain(t):
            nc.scalar.copy(win_y[t][:, :S], h_acc[t][:])

        def fetch_a(t):
            pa[t] = new("first", 2)
            nc.vector.tensor_copy(pa[t][:], win_y[t][:].indirect(l5[:]))

        def fetch_both(t):
            both[t] = new("second", 3)
            nc.vector.tensor_tensor(both[t][:], win_y[t][:].indirect(l6[:]), pa[t][:], ALU.add)

        def plain_d(t):
            diff = new("diff")
            nc.vector.scalar_tensor_tensor(diff[:], pa[t][:], 2.0, both[t][:], ALU.mult, ALU.subtract)
            sq_d[t] = new("dc", 3)
            nc.scalar.activation(sq_d[t][:], diff[:], ACT.Square, scale=SC_D)

        def plain_m(t):
            mid = new("diff")
            nc.vector.scalar_tensor_tensor(mid[:], win_y[t][:, :S], -5.0 / 3.0, both[t][:], ALU.mult, ALU.add)
            sq_m[t] = new("dc", 3) if t < last else new("less", 3)
            nc.scalar.activation(sq_m[t][:], mid[:], ACT.Square, scale=SC_M)

        def plain_n(t):
            num[t] = new("num", 4)
            nc.vector.scalar_tensor_tensor(num[t][:], win_y[t][:, :S], -11.0 / 5.0, both[t][:], ALU.mult, ALU.add)

        def plain_q(t, pieces):
            q = new("m1c", 3)
            root[t] = new("root", 3)
            for c0, c1 in pieces:
                nc.vector.tensor_tensor(q[:, c0:c1], sq_d[t][:, c0:c1], sq_m[t][:, c0:c1], ALU.add)
                nc.scalar.activation(root[t][:, c0:c1], q[:, c0:c1], ACT.Abs_reciprocal_sqrt, bias=quarter[:])

        leave(0)
        fetch1(0)
        leave(1)
        fetch2(0)
        fetch1(1)
        leave_extra(0)
        numer(0)
        leave_plain(2)
        spread_d(0)
        fetch2(1)
        leave_extra(1)
        fetch_a(2)
        spread_m(0)
        numer(1)
        leave_plain(3)
        spread_d(1)
        fetch_both(2)
        fetch_a(3)
        spread_q(0)
        plain_d(2)
        plain_m(2)
        spread_m(1)
        fetch_both(3)
        plain_n(2)
        spread_q(1)
        plain_d(3)
        plain_m(3)
        plain_q(2, [(0, S)])
        finish(0)
        plain_n(3)
        finish(1)
        plain_q(3, [(0, HALF), (HALF, S)])
        finish(2)
        for c0 in (0, HALF):
            finish(last, c0, c0 + HALF)
